import numpy as np
import ml_dtypes


def mxq(x, axis, fmt="e4m3"):
    dtype, down = {"e4m3": (ml_dtypes.float8_e4m3fn, 7), "e5m2": (ml_dtypes.float8_e5m2, 14)}[fmt]
    v = np.moveaxis(np.asarray(x, np.float32).astype(ml_dtypes.bfloat16).astype(np.float64), axis, -1)
    blocks = v.reshape(v.shape[:-1] + (-1, 32))
    amax = np.abs(blocks).max(-1, keepdims=True)
    byte = np.maximum(np.where(amax > 0, np.frexp(amax)[1] - 1 + 127, 0) - down, 1)
    scale = np.exp2(byte - 127.0)
    codes = (blocks / scale).astype(np.float32).astype(dtype).astype(np.float64)
    return np.moveaxis((codes * scale).reshape(v.shape), -1, axis)


WIDE = False


def mx_kscale(k):
    if not WIDE:
        return np.ones(k)
    levels = np.array([10, -10, 5, -5, 0])
    if k % 512:
        return np.exp2(np.random.permutation(np.resize(levels, k // 32))).repeat(32)
    a = np.empty((k // 512, 16))
    for p in range(k // 512):
        a[p, :8] = np.random.permutation(np.resize(levels, 8))
        for g in range(8):
            far = levels[np.abs(levels - a[p, g]) >= 10]
            a[p, g + 8] = far[np.random.randint(len(far))]
    return np.exp2(a.ravel()).repeat(32)


def f64(x):
    return np.asarray(x).astype(np.float64)


def striped(idx):
    return np.tile(np.asarray(idx).reshape(-1, 16).T, (8, 1)).astype(np.uint16)


def unstriped(offs):
    return offs[:16].T.reshape(-1).astype(np.int64)


B, N, T, D, DV, NQ = 1, 512, 2048, 256, 512, 512


def setup_inputs():
    n = np.random.standard_normal
    idx = np.random.permutation(T)[:B * N]
    s = mx_kscale(DV)[:, None]
    z = mx_kscale(NQ)[:, None]
    p = np.exp(n((B, NQ, N)))
    p = p / p.mean(2, keepdims=True)
    return {
        "doT": (n((B, DV, NQ)) * s / np.sqrt(DV)).astype(np.float32),
        "vT": (n((DV, T)) / s).astype(np.float32),
        "p": (p * z / np.sqrt(NQ)).astype(np.float32),
        "delta": (0.3 * n((B, NQ, 1))).astype(np.float32),
        "qm": (n((B, NQ, D)) / z).astype(np.float32),
        "offs": striped(idx),
    }


def reference(doT, vT, p, delta, qm, offs):
    idx = unstriped(offs)
    pick = lambda x: x[:, idx].reshape(x.shape[0], B, N).transpose(1, 0, 2)
    dp = mxq(f64(doT), 1, "e4m3").transpose(0, 2, 1) @ mxq(pick(f64(vT)), 1, "e4m3")
    ds = f64(p) * (dp - f64(delta))
    dk = mxq(f64(qm), 1, "e4m3").transpose(0, 2, 1) @ mxq(ds, 1, "e4m3")
    out = np.zeros((D, T))
    out[:, idx] = dk.transpose(1, 0, 2).reshape(D, B * N)
    return out

@@ -1,0 +1,166 @@
+from contextlib import ExitStack
+
+import concourse.mybir as mybir
+
+NQ, N, T, D, DV = 512, 512, 2048, 256, 512
+FLOPS = 2 * NQ * N * DV + 2 * D * N * NQ
+
+F32 = mybir.dt.float32
+BF16 = mybir.dt.bfloat16
+U32 = mybir.dt.uint32
+U16 = mybir.dt.uint16
+U8 = mybir.dt.uint8
+FP8X4 = mybir.dt.float8_e4m3fn_x4
+MULT = mybir.AluOpType.mult
+SUB = mybir.AluOpType.subtract
+IDENT = mybir.ActivationFunctionType.Identity
+
+P = 128
+J = 4
+HALF = N // 2
+M_VECTOR = 88
+
+
+def tile_attend_bwd_kernel(tc, doT, vT, p, delta, qm, offs, out):
+    nc = tc.nc
+    with ExitStack() as ctx:
+        keep = ctx.enter_context(tc.tile_pool(name="keep", bufs=1))
+        psum = ctx.enter_context(tc.psum_pool(name="psum", bufs=1))
+
+        offsets = keep.tile([P, N // 16], U16, name="offsets")
+        nc.sync.dma_start(offsets[:], offs)
+        v_view = vT.rearrange("(p t) n -> p t n", t=J)
+        v_planes = []
+        for t in range(J):
+            plane = keep.tile([P, T], F32, name=f"plane{t}")
+            nc.sync.dma_start(plane[:], v_view[:, t, :])
+            v_planes.append(plane)
+        do_raw = keep.tile([P, J, NQ], F32, name="do_raw")
+        nc.sync.dma_start(do_raw[:], doT[0].rearrange("(p j) q -> p j q", j=J))
+        q_raw = keep.tile([P, J, D], F32, name="q_raw")
+        nc.sync.dma_start(q_raw[:], qm[0].rearrange("(p t) d -> p t d", t=J))
+        p_view = p[0].rearrange("(p t) n -> p t n", t=J)
+        p_halves = []
+        for h in range(2):
+            p_half = keep.tile([P, J, HALF], F32, name=f"p_half{h}")
+            nc.sync.dma_start(p_half[:], p_view[:, :, h * HALF : (h + 1) * HALF])
+            p_halves.append(p_half)
+        delta_sb = keep.tile([P, J], F32, name="delta_sb")
+        nc.scalar.dma_start(delta_sb[:], delta[0].rearrange("(p t) o -> p (t o)", t=J))
+
+        windows = []
+        for b in range(2):
+            window = keep.tile([P, T], F32, name=f"window{b}")
+            (nc.vector if b == 0 else nc.gpsimd).memset(window[:], 0.0)
+            windows.append(window)
+        neg_delta = keep.tile([P, J], F32, name="neg_delta")
+        nc.scalar.activation(neg_delta[:], delta_sb[:], IDENT, scale=-1.0)
+
+        v_grouped = keep.tile([P, N, J], BF16, name="v_grouped", align_bytes=64)
+        for t in range(J):
+            nc.vector.tensor_copy(v_grouped[:, :, t], v_planes[t][:].indirect(offsets[:]))
+        v_codes = keep.tile([P, N], U32, name="v_codes", align_bytes=64)
+        v_scales = keep.tile([P, N], U8, name="v_scales", align_bytes=64)
+        nc.vector.quantize_mx(
+            out=v_codes[:].bitcast(FP8X4), scales=v_scales[:], in_=v_grouped[:].rearrange("p n t -> p (n t)")
+        )
+
+        do_grouped = keep.tile([P, J, P, J], BF16, name="do_grouped", align_bytes=64)
+        do_dst = do_grouped[:].rearrange("p t m j -> p m t j")
+        do_src = do_raw[:].rearrange("p j (m t) -> p m t j", t=J)
+        nc.vector.tensor_copy(do_dst[:, :M_VECTOR], do_src[:, :M_VECTOR])
+        nc.scalar.copy(do_dst[:, M_VECTOR:], do_src[:, M_VECTOR:])
+        do_flat = do_grouped[:].rearrange("p t m j -> p (t m j)")
+        do_codes = keep.tile([P, NQ], U32, name="do_codes", align_bytes=64)
+        do_scales = keep.tile([P, NQ], U8, name="do_scales", align_bytes=64)
+        for h in range(2):
+            w = slice(h * 256, (h + 1) * 256)
+            nc.vector.quantize_mx(
+                out=do_codes[:, w].bitcast(FP8X4), scales=do_scales[:, w], in_=do_flat[:, h * 1024 : (h + 1) * 1024]
+            )
+
+        q_grouped = keep.tile([P, D, J], BF16, name="q_grouped", align_bytes=64)
+        nc.scalar.copy(q_grouped[:], q_raw[:].rearrange("p t d -> p d t"))
+        q_codes = keep.tile([P, D], U32, name="q_codes", align_bytes=64)
+        q_scales = keep.tile([P, D], U8, name="q_scales", align_bytes=64)
+
+        centred = []
+        for h in range(2):
+            cols = slice(h * HALF, (h + 1) * HALF)
+            c_sb = keep.tile([P, J, HALF], F32, name=f"centred{h}")
+            for t in range(J):
+                dp = psum.tile([P, HALF], F32, name=f"bank{4 * h + t}")
+                q_cols = slice(t * P, (t + 1) * P)
+                nc.tensor.matmul_mx(
+                    out=dp[:],
+                    lhsT=do_codes[:, q_cols].bitcast(FP8X4),
+                    lhsT_scale=do_scales[:, q_cols],
+                    rhs=v_codes[:, cols].bitcast(FP8X4),
+                    rhs_scale=v_scales[:, cols],
+                    start=True,
+                    stop=True,
+                )
+                if (h, t) in ((0, 0), (0, 1), (0, 2)):
+                    nc.vector.tensor_scalar(c_sb[:, t, :], dp[:], delta_sb[:, t : t + 1], None, SUB)
+                else:
+                    nc.scalar.activation(c_sb[:, t, :], dp[:], IDENT, bias=neg_delta[:, t : t + 1])
+            centred.append(c_sb)
+
+        ds_grouped = []
+        ds_codes = []
+        ds_scales = []
+        for h in range(2):
+            ds_grouped.append(keep.tile([P, HALF, J], BF16, name=f"ds_grouped{h}", align_bytes=64))
+            ds_codes.append(keep.tile([P, HALF], U32, name=f"ds_codes{h}", align_bytes=64))
+            ds_scales.append(keep.tile([P, HALF], U8, name=f"ds_scales{h}", align_bytes=64))
+
+        def weigh(h):
+            nc.vector.tensor_tensor(
+                ds_grouped[h][:].rearrange("p (c i) t -> p c t i", i=4),
+                centred[h][:].rearrange("p t (c i) -> p c t i", i=4),
+                p_halves[h][:].rearrange("p t (c i) -> p c t i", i=4),
+                MULT,
+            )
+
+        def quantise_ds(h):
+            nc.vector.quantize_mx(
+                out=ds_codes[h][:].bitcast(FP8X4),
+                scales=ds_scales[h][:],
+                in_=ds_grouped[h][:].rearrange("p n t -> p (n t)"),
+            )
+
+        def multiply(h):
+            result = []
+            for b in range(2):
+                dk = psum.tile([P, HALF], F32, name=f"bank{2 * h + b}")
+                d_cols = slice(b * P, (b + 1) * P)
+                nc.tensor.matmul_mx(
+                    out=dk[:],
+                    lhsT=q_codes[:, d_cols].bitcast(FP8X4),
+                    lhsT_scale=q_scales[:, d_cols],
+                    rhs=ds_codes[h][:].bitcast(FP8X4),
+                    rhs_scale=ds_scales[h][:],
+                    start=True,
+                    stop=True,
+                )
+                dk_sb = keep.tile([P, HALF], F32, name=f"dk_sb{h}{b}")
+                nc.scalar.copy(dk_sb[:], dk[:])
+                result.append(dk_sb)
+            return result
+
+        def scatter(h, b, dk_sb):
+            nc.vector.tensor_copy(windows[b][:].indirect(offsets[:, h * 16 : (h + 1) * 16]), dk_sb[:])
+
+        weigh(0)
+        nc.vector.quantize_mx(
+            out=q_codes[:].bitcast(FP8X4), scales=q_scales[:], in_=q_grouped[:].rearrange("p d t -> p (d t)")
+        )
+        quantise_ds(0)
+        dk0 = multiply(0)
+        weigh(1)
+        quantise_ds(1)
+        dk1 = multiply(1)
+        for b in range(2):
+            scatter(0, b, dk0[b])
+            scatter(1, b, dk1[b])
+            nc.sync.dma_start(out[b * P : (b + 1) * P, :], windows[b][:])

@@ -28,13 +28,14 @@ def tile_attend_bwd_kernel(tc, doT, vT, p, delta, qm, offs, out):
         psum = ctx.enter_context(tc.psum_pool(name="psum", bufs=1))
 
         offsets = keep.tile([P, N // 16], U16, name="offsets")
-        nc.sync.dma_start(offsets[:], offs)
         v_view = vT.rearrange("(p t) n -> p t n", t=J)
         v_planes = []
         for t in range(J):
             plane = keep.tile([P, T], F32, name=f"plane{t}")
             nc.sync.dma_start(plane[:], v_view[:, t, :])
             v_planes.append(plane)
+            if t == 0:
+                nc.sync.dma_start(offsets[:], offs)
         do_raw = keep.tile([P, J, NQ], F32, name="do_raw")
         nc.sync.dma_start(do_raw[:], doT[0].rearrange("(p j) q -> p j q", j=J))
         q_raw = keep.tile([P, J, D], F32, name="q_raw")
@@ -84,6 +85,10 @@ def tile_attend_bwd_kernel(tc, doT, vT, p, delta, qm, offs, out):
         q_codes = keep.tile([P, D], U32, name="q_codes", align_bytes=64)
         q_scales = keep.tile([P, D], U8, name="q_scales", align_bytes=64)
 
+        nc.vector.quantize_mx(
+            out=q_codes[:].bitcast(FP8X4), scales=q_scales[:], in_=q_grouped[:].rearrange("p d t -> p (d t)")
+        )
+
         centred = []
         for h in range(2):
             cols = slice(h * HALF, (h + 1) * HALF)
@@ -100,7 +105,7 @@ def tile_attend_bwd_kernel(tc, doT, vT, p, delta, qm, offs, out):
                     start=True,
                     stop=True,
                 )
-                if (h, t) in ((0, 0), (0, 1), (0, 2)):
+                if h == 0:
                     nc.vector.tensor_scalar(c_sb[:, t, :], dp[:], delta_sb[:, t : t + 1], None, SUB)
                 else:
                     nc.scalar.activation(c_sb[:, t, :], dp[:], IDENT, bias=neg_delta[:, t : t + 1])
@@ -110,11 +115,10 @@ def tile_attend_bwd_kernel(tc, doT, vT, p, delta, qm, offs, out):
         ds_codes = []
         ds_scales = []
         for h in range(2):
-            ds_grouped.append(keep.tile([P, HALF, J], BF16, name=f"ds_grouped{h}", align_bytes=64))
-            ds_codes.append(keep.tile([P, HALF], U32, name=f"ds_codes{h}", align_bytes=64))
             ds_scales.append(keep.tile([P, HALF], U8, name=f"ds_scales{h}", align_bytes=64))
 
         def weigh(h):
+            ds_grouped.append(keep.tile([P, HALF, J], BF16, name="ds_grouped", align_bytes=64))
             nc.vector.tensor_tensor(
                 ds_grouped[h][:].rearrange("p (c i) t -> p c t i", i=4),
                 centred[h][:].rearrange("p t (c i) -> p c t i", i=4),
@@ -123,6 +127,7 @@ def tile_attend_bwd_kernel(tc, doT, vT, p, delta, qm, offs, out):
             )
 
         def quantise_ds(h):
+            ds_codes.append(keep.tile([P, HALF], U32, name=f"ds_codes{h}", align_bytes=64))
             nc.vector.quantize_mx(
                 out=ds_codes[h][:].bitcast(FP8X4),
                 scales=ds_scales[h][:],
@@ -132,7 +137,7 @@ def tile_attend_bwd_kernel(tc, doT, vT, p, delta, qm, offs, out):
         def multiply(h):
             result = []
             for b in range(2):
-                dk = psum.tile([P, HALF], F32, name=f"bank{2 * h + b}")
+                dk = psum.tile([P, HALF], F32, name=("bank0", "bank0", "bank1", "bank2")[2 * h + b])
                 d_cols = slice(b * P, (b + 1) * P)
                 nc.tensor.matmul_mx(
                     out=dk[:],
@@ -152,15 +157,14 @@ def tile_attend_bwd_kernel(tc, doT, vT, p, delta, qm, offs, out):
             nc.vector.tensor_copy(windows[b][:].indirect(offsets[:, h * 16 : (h + 1) * 16]), dk_sb[:])
 
         weigh(0)
-        nc.vector.quantize_mx(
-            out=q_codes[:].bitcast(FP8X4), scales=q_scales[:], in_=q_grouped[:].rearrange("p d t -> p (d t)")
-        )
         quantise_ds(0)
         dk0 = multiply(0)
         weigh(1)
+        scatter(0, 0, dk0[0])
         quantise_ds(1)
         dk1 = multiply(1)
-        for b in range(2):
-            scatter(0, b, dk0[b])
-            scatter(1, b, dk1[b])
-            nc.sync.dma_start(out[b * P : (b + 1) * P, :], windows[b][:])
+        scatter(0, 1, dk0[1])
+        scatter(1, 0, dk1[0])
+        nc.sync.dma_start(out[0:P, :], windows[0][:])
+        scatter(1, 1, dk1[1])
+        nc.sync.dma_start(out[P : 2 * P, :], windows[1][:])

@@ -13,12 +13,12 @@ U8 = mybir.dt.uint8
 FP8X4 = mybir.dt.float8_e4m3fn_x4
 MULT = mybir.AluOpType.mult
 SUB = mybir.AluOpType.subtract
-IDENT = mybir.ActivationFunctionType.Identity
 
 P = 128
 J = 4
 HALF = N // 2
 M_VECTOR = 88
+B_VECTOR = 144
 
 
 def tile_attend_bwd_kernel(tc, doT, vT, p, delta, qm, offs, out):
@@ -54,21 +54,28 @@ def tile_attend_bwd_kernel(tc, doT, vT, p, delta, qm, offs, out):
             window = keep.tile([P, T], F32, name=f"window{b}")
             (nc.vector if b == 0 else nc.gpsimd).memset(window[:], 0.0)
             windows.append(window)
-        neg_delta = keep.tile([P, J], F32, name="neg_delta")
-        nc.scalar.activation(neg_delta[:], delta_sb[:], IDENT, scale=-1.0)
 
         v_grouped = keep.tile([P, N, J], BF16, name="v_grouped", align_bytes=64)
-        for t in range(J):
+        for t in range(J - 1):
             nc.vector.tensor_copy(v_grouped[:, :, t], v_planes[t][:].indirect(offsets[:]))
+        for h in range(2):
+            nc.vector.tensor_copy(
+                v_grouped[:, h * HALF : (h + 1) * HALF, J - 1],
+                v_planes[J - 1][:].indirect(offsets[:, h * 16 : (h + 1) * 16]),
+            )
         v_codes = keep.tile([P, N], U32, name="v_codes", align_bytes=64)
         v_scales = keep.tile([P, N], U8, name="v_scales", align_bytes=64)
-        nc.vector.quantize_mx(
-            out=v_codes[:].bitcast(FP8X4), scales=v_scales[:], in_=v_grouped[:].rearrange("p n t -> p (n t)")
-        )
+        for h in range(2):
+            cols = slice(h * HALF, (h + 1) * HALF)
+            nc.vector.quantize_mx(
+                out=v_codes[:, cols].bitcast(FP8X4),
+                scales=v_scales[:, cols],
+                in_=v_grouped[:, cols, :].rearrange("p n t -> p (n t)"),
+            )
 
         do_grouped = keep.tile([P, J, P, J], BF16, name="do_grouped", align_bytes=64)
-        do_dst = do_grouped[:].rearrange("p t m j -> p m t j")
-        do_src = do_raw[:].rearrange("p j (m t) -> p m t j", t=J)
+        do_dst = do_grouped[:].rearrange("p t m j -> p m j t")
+        do_src = do_raw[:].rearrange("p j (m t) -> p m j t", t=J)
         nc.vector.tensor_copy(do_dst[:, :M_VECTOR], do_src[:, :M_VECTOR])
         nc.scalar.copy(do_dst[:, M_VECTOR:], do_src[:, M_VECTOR:])
         do_flat = do_grouped[:].rearrange("p t m j -> p (t m j)")
@@ -81,7 +88,9 @@ def tile_attend_bwd_kernel(tc, doT, vT, p, delta, qm, offs, out):
             )
 
         q_grouped = keep.tile([P, D, J], BF16, name="q_grouped", align_bytes=64)
-        nc.scalar.copy(q_grouped[:], q_raw[:].rearrange("p t d -> p d t"))
+        nc.scalar.copy(
+            q_grouped[:].rearrange("p (c i) t -> p c t i", i=4), q_raw[:].rearrange("p t (c i) -> p c t i", i=4)
+        )
         q_codes = keep.tile([P, D], U32, name="q_codes", align_bytes=64)
         q_scales = keep.tile([P, D], U8, name="q_scales", align_bytes=64)
 
@@ -89,10 +98,12 @@ def tile_attend_bwd_kernel(tc, doT, vT, p, delta, qm, offs, out):
             out=q_codes[:].bitcast(FP8X4), scales=q_scales[:], in_=q_grouped[:].rearrange("p d t -> p (d t)")
         )
 
-        centred = []
+        part = [keep.tile([P, J, HALF], F32, name=f"part{h}") for h in range(2)]
+        ds_grouped = [keep.tile([P, HALF, J], BF16, name=f"ds_grouped{h}", align_bytes=64) for h in range(2)]
+        ds_codes = [keep.tile([P, HALF], U32, name=f"ds_codes{h}", align_bytes=64) for h in range(2)]
+        ds_scales = [keep.tile([P, HALF], U8, name=f"ds_scales{h}", align_bytes=64) for h in range(2)]
         for h in range(2):
             cols = slice(h * HALF, (h + 1) * HALF)
-            c_sb = keep.tile([P, J, HALF], F32, name=f"centred{h}")
             for t in range(J):
                 dp = psum.tile([P, HALF], F32, name=f"bank{4 * h + t}")
                 q_cols = slice(t * P, (t + 1) * P)
@@ -105,40 +116,30 @@ def tile_attend_bwd_kernel(tc, doT, vT, p, delta, qm, offs, out):
                     start=True,
                     stop=True,
                 )
-                if h == 0:
-                    nc.vector.tensor_scalar(c_sb[:, t, :], dp[:], delta_sb[:, t : t + 1], None, SUB)
-                else:
-                    nc.scalar.activation(c_sb[:, t, :], dp[:], IDENT, bias=neg_delta[:, t : t + 1])
-            centred.append(c_sb)
+                nc.vector.scalar_tensor_tensor(
+                    part[h][:, t, :], dp[:], delta_sb[:, t : t + 1], p_halves[h][:, t, :], SUB, MULT
+                )
 
-        ds_grouped = []
-        ds_codes = []
-        ds_scales = []
-        for h in range(2):
-            ds_scales.append(keep.tile([P, HALF], U8, name=f"ds_scales{h}", align_bytes=64))
-
-        def weigh(h):
-            ds_grouped.append(keep.tile([P, HALF, J], BF16, name="ds_grouped", align_bytes=64))
-            nc.vector.tensor_tensor(
-                ds_grouped[h][:].rearrange("p (c i) t -> p c t i", i=4),
-                centred[h][:].rearrange("p t (c i) -> p c t i", i=4),
-                p_halves[h][:].rearrange("p t (c i) -> p c t i", i=4),
-                MULT,
+        def group(copy, h, first, last):
+            copy(
+                ds_grouped[h][:, first:last].rearrange("p (c i) t -> p c t i", i=4),
+                part[h][:, :, first:last].rearrange("p t (c i) -> p c t i", i=4),
             )
 
-        def quantise_ds(h):
-            ds_codes.append(keep.tile([P, HALF], U32, name=f"ds_codes{h}", align_bytes=64))
+        group(nc.scalar.copy, 0, 0, HALF)
+        group(nc.vector.tensor_copy, 1, HALF - B_VECTOR, HALF)
+        group(nc.scalar.copy, 1, 0, HALF - B_VECTOR)
+        for h in range(2):
             nc.vector.quantize_mx(
                 out=ds_codes[h][:].bitcast(FP8X4),
                 scales=ds_scales[h][:],
                 in_=ds_grouped[h][:].rearrange("p n t -> p (n t)"),
             )
 
-        def multiply(h):
-            result = []
-            for b in range(2):
-                dk = psum.tile([P, HALF], F32, name=("bank0", "bank0", "bank1", "bank2")[2 * h + b])
-                d_cols = slice(b * P, (b + 1) * P)
+        for b in range(2):
+            d_cols = slice(b * P, (b + 1) * P)
+            for h in range(2):
+                dk = psum.tile([P, HALF], F32, name="bank0" if b == h == 0 else "bank1")
                 nc.tensor.matmul_mx(
                     out=dk[:],
                     lhsT=q_codes[:, d_cols].bitcast(FP8X4),
@@ -150,21 +151,5 @@ def tile_attend_bwd_kernel(tc, doT, vT, p, delta, qm, offs, out):
                 )
                 dk_sb = keep.tile([P, HALF], F32, name=f"dk_sb{h}{b}")
                 nc.scalar.copy(dk_sb[:], dk[:])
-                result.append(dk_sb)
-            return result
-
-        def scatter(h, b, dk_sb):
-            nc.vector.tensor_copy(windows[b][:].indirect(offsets[:, h * 16 : (h + 1) * 16]), dk_sb[:])
-
-        weigh(0)
-        quantise_ds(0)
-        dk0 = multiply(0)
-        weigh(1)
-        scatter(0, 0, dk0[0])
-        quantise_ds(1)
-        dk1 = multiply(1)
-        scatter(0, 1, dk0[1])
-        scatter(1, 0, dk1[0])
-        nc.sync.dma_start(out[0:P, :], windows[0][:])
-        scatter(1, 1, dk1[1])
-        nc.sync.dma_start(out[P : 2 * P, :], windows[1][:])
+                nc.vector.tensor_copy(windows[b][:].indirect(offsets[:, h * 16 : (h + 1) * 16]), dk_sb[:])
+            nc.sync.dma_start(out[b * P : (b + 1) * P, :], windows[b][:])

@@ -38,16 +38,17 @@ def tile_attend_bwd_kernel(tc, doT, vT, p, delta, qm, offs, out):
                 nc.sync.dma_start(offsets[:], offs)
         do_raw = keep.tile([P, J, NQ], F32, name="do_raw")
         nc.sync.dma_start(do_raw[:], doT[0].rearrange("(p j) q -> p j q", j=J))
-        q_raw = keep.tile([P, J, D], F32, name="q_raw")
-        nc.sync.dma_start(q_raw[:], qm[0].rearrange("(p t) d -> p t d", t=J))
+        delta_sb = keep.tile([P, J], F32, name="delta_sb")
+        nc.sync.dma_start(delta_sb[:], delta[0].rearrange("(p t) o -> p (t o)", t=J))
         p_view = p[0].rearrange("(p t) n -> p t n", t=J)
         p_halves = []
         for h in range(2):
             p_half = keep.tile([P, J, HALF], F32, name=f"p_half{h}")
             nc.sync.dma_start(p_half[:], p_view[:, :, h * HALF : (h + 1) * HALF])
             p_halves.append(p_half)
-        delta_sb = keep.tile([P, J], F32, name="delta_sb")
-        nc.scalar.dma_start(delta_sb[:], delta[0].rearrange("(p t) o -> p (t o)", t=J))
+            if h == 0:
+                q_raw = keep.tile([P, J, D], F32, name="q_raw")
+                nc.sync.dma_start(q_raw[:], qm[0].rearrange("(p t) d -> p t d", t=J))
 
         windows = []
         for b in range(2):
@@ -136,9 +137,11 @@ def tile_attend_bwd_kernel(tc, doT, vT, p, delta, qm, offs, out):
                 in_=ds_grouped[h][:].rearrange("p n t -> p (n t)"),
             )
 
+        dk_sb = [keep.tile([P, N], F32, name=f"dk_sb{b}") for b in range(2)]
         for b in range(2):
             d_cols = slice(b * P, (b + 1) * P)
             for h in range(2):
+                cols = slice(h * HALF, (h + 1) * HALF)
                 dk = psum.tile([P, HALF], F32, name="bank0" if b == h == 0 else "bank1")
                 nc.tensor.matmul_mx(
                     out=dk[:],
@@ -149,7 +152,11 @@ def tile_attend_bwd_kernel(tc, doT, vT, p, delta, qm, offs, out):
                     start=True,
                     stop=True,
                 )
-                dk_sb = keep.tile([P, HALF], F32, name=f"dk_sb{h}{b}")
-                nc.scalar.copy(dk_sb[:], dk[:])
-                nc.vector.tensor_copy(windows[b][:].indirect(offsets[:, h * 16 : (h + 1) * 16]), dk_sb[:])
+                nc.scalar.copy(dk_sb[b][:, cols], dk[:])
+                if b == 0:
+                    nc.vector.tensor_copy(
+                        windows[b][:].indirect(offsets[:, h * 16 : (h + 1) * 16]), dk_sb[b][:, cols]
+                    )
+            if b == 1:
+                nc.vector.tensor_copy(windows[b][:].indirect(offsets[:]), dk_sb[b][:])
             nc.sync.dma_start(out[b * P : (b + 1) * P, :], windows[b][:])

from contextlib import ExitStack

import concourse.mybir as mybir

NQ, N, T, D, DV = 512, 512, 2048, 256, 512
FLOPS = 2 * NQ * N * DV + 2 * D * N * NQ

F32 = mybir.dt.float32
BF16 = mybir.dt.bfloat16
U32 = mybir.dt.uint32
U16 = mybir.dt.uint16
U8 = mybir.dt.uint8
FP8X4 = mybir.dt.float8_e4m3fn_x4
MULT = mybir.AluOpType.mult
SUB = mybir.AluOpType.subtract

P = 128
J = 4
HALF = N // 2
M_VECTOR = 88
B_VECTOR = 144


def tile_attend_bwd_kernel(tc, doT, vT, p, delta, qm, offs, out):
    nc = tc.nc
    with ExitStack() as ctx:
        keep = ctx.enter_context(tc.tile_pool(name="keep", bufs=1))
        psum = ctx.enter_context(tc.psum_pool(name="psum", bufs=1))

        offsets = keep.tile([P, N // 16], U16, name="offsets")
        v_view = vT.rearrange("(p t) n -> p t n", t=J)
        v_planes = []
        for t in range(J):
            plane = keep.tile([P, T], F32, name=f"plane{t}")
            nc.sync.dma_start(plane[:], v_view[:, t, :])
            v_planes.append(plane)
            if t == 0:
                nc.sync.dma_start(offsets[:], offs)
        do_raw = keep.tile([P, J, NQ], F32, name="do_raw")
        nc.sync.dma_start(do_raw[:], doT[0].rearrange("(p j) q -> p j q", j=J))
        delta_sb = keep.tile([P, J], F32, name="delta_sb")
        nc.sync.dma_start(delta_sb[:], delta[0].rearrange("(p t) o -> p (t o)", t=J))
        p_view = p[0].rearrange("(p t) n -> p t n", t=J)
        p_halves = []
        for h in range(2):
            p_half = keep.tile([P, J, HALF], F32, name=f"p_half{h}")
            nc.sync.dma_start(p_half[:], p_view[:, :, h * HALF : (h + 1) * HALF])
            p_halves.append(p_half)
            if h == 0:
                q_raw = keep.tile([P, J, D], F32, name="q_raw")
                nc.sync.dma_start(q_raw[:], qm[0].rearrange("(p t) d -> p t d", t=J))

        windows = []
        for b in range(2):
            window = keep.tile([P, T], F32, name=f"window{b}")
            (nc.vector if b == 0 else nc.gpsimd).memset(window[:], 0.0)
            windows.append(window)

        v_grouped = keep.tile([P, N, J], BF16, name="v_grouped", align_bytes=64)
        for t in range(J - 1):
            nc.vector.tensor_copy(v_grouped[:, :, t], v_planes[t][:].indirect(offsets[:]))
        for h in range(2):
            nc.vector.tensor_copy(
                v_grouped[:, h * HALF : (h + 1) * HALF, J - 1],
                v_planes[J - 1][:].indirect(offsets[:, h * 16 : (h + 1) * 16]),
            )
        v_codes = keep.tile([P, N], U32, name="v_codes", align_bytes=64)
        v_scales = keep.tile([P, N], U8, name="v_scales", align_bytes=64)
        for h in range(2):
            cols = slice(h * HALF, (h + 1) * HALF)
            nc.vector.quantize_mx(
                out=v_codes[:, cols].bitcast(FP8X4),
                scales=v_scales[:, cols],
                in_=v_grouped[:, cols, :].rearrange("p n t -> p (n t)"),
            )

        do_grouped = keep.tile([P, J, P, J], BF16, name="do_grouped", align_bytes=64)
        do_dst = do_grouped[:].rearrange("p t m j -> p m j t")
        do_src = do_raw[:].rearrange("p j (m t) -> p m j t", t=J)
        nc.vector.tensor_copy(do_dst[:, :M_VECTOR], do_src[:, :M_VECTOR])
        nc.scalar.copy(do_dst[:, M_VECTOR:], do_src[:, M_VECTOR:])
        do_flat = do_grouped[:].rearrange("p t m j -> p (t m j)")
        do_codes = keep.tile([P, NQ], U32, name="do_codes", align_bytes=64)
        do_scales = keep.tile([P, NQ], U8, name="do_scales", align_bytes=64)
        for h in range(2):
            w = slice(h * 256, (h + 1) * 256)
            nc.vector.quantize_mx(
                out=do_codes[:, w].bitcast(FP8X4), scales=do_scales[:, w], in_=do_flat[:, h * 1024 : (h + 1) * 1024]
            )

        q_grouped = keep.tile([P, D, J], BF16, name="q_grouped", align_bytes=64)
        nc.scalar.copy(
            q_grouped[:].rearrange("p (c i) t -> p c t i", i=4), q_raw[:].rearrange("p t (c i) -> p c t i", i=4)
        )
        q_codes = keep.tile([P, D], U32, name="q_codes", align_bytes=64)
        q_scales = keep.tile([P, D], U8, name="q_scales", align_bytes=64)

        nc.vector.quantize_mx(
            out=q_codes[:].bitcast(FP8X4), scales=q_scales[:], in_=q_grouped[:].rearrange("p d t -> p (d t)")
        )

        part = [keep.tile([P, J, HALF], F32, name=f"part{h}") for h in range(2)]
        ds_grouped = [keep.tile([P, HALF, J], BF16, name=f"ds_grouped{h}", align_bytes=64) for h in range(2)]
        ds_codes = [keep.tile([P, HALF], U32, name=f"ds_codes{h}", align_bytes=64) for h in range(2)]
        ds_scales = [keep.tile([P, HALF], U8, name=f"ds_scales{h}", align_bytes=64) for h in range(2)]
        for h in range(2):
            cols = slice(h * HALF, (h + 1) * HALF)
            for t in range(J):
                dp = psum.tile([P, HALF], F32, name=f"bank{4 * h + t}")
                q_cols = slice(t * P, (t + 1) * P)
                nc.tensor.matmul_mx(
                    out=dp[:],
                    lhsT=do_codes[:, q_cols].bitcast(FP8X4),
                    lhsT_scale=do_scales[:, q_cols],
                    rhs=v_codes[:, cols].bitcast(FP8X4),
                    rhs_scale=v_scales[:, cols],
                    start=True,
                    stop=True,
                )
                nc.vector.scalar_tensor_tensor(
                    part[h][:, t, :], dp[:], delta_sb[:, t : t + 1], p_halves[h][:, t, :], SUB, MULT
                )

        def group(copy, h, first, last):
            copy(
                ds_grouped[h][:, first:last].rearrange("p (c i) t -> p c t i", i=4),
                part[h][:, :, first:last].rearrange("p t (c i) -> p c t i", i=4),
            )

        group(nc.scalar.copy, 0, 0, HALF)
        group(nc.vector.tensor_copy, 1, HALF - B_VECTOR, HALF)
        group(nc.scalar.copy, 1, 0, HALF - B_VECTOR)
        for h in range(2):
            nc.vector.quantize_mx(
                out=ds_codes[h][:].bitcast(FP8X4),
                scales=ds_scales[h][:],
                in_=ds_grouped[h][:].rearrange("p n t -> p (n t)"),
            )

        dk_sb = [keep.tile([P, N], F32, name=f"dk_sb{b}") for b in range(2)]
        for b in range(2):
            d_cols = slice(b * P, (b + 1) * P)
            for h in range(2):
                cols = slice(h * HALF, (h + 1) * HALF)
                dk = psum.tile([P, HALF], F32, name="bank0" if b == h == 0 else "bank1")
                nc.tensor.matmul_mx(
                    out=dk[:],
                    lhsT=q_codes[:, d_cols].bitcast(FP8X4),
                    lhsT_scale=q_scales[:, d_cols],
                    rhs=ds_codes[h][:].bitcast(FP8X4),
                    rhs_scale=ds_scales[h][:],
                    start=True,
                    stop=True,
                )
                nc.scalar.copy(dk_sb[b][:, cols], dk[:])
                if b == 0:
                    nc.vector.tensor_copy(
                        windows[b][:].indirect(offsets[:, h * 16 : (h + 1) * 16]), dk_sb[b][:, cols]
                    )
            if b == 1:
                nc.vector.tensor_copy(windows[b][:].indirect(offsets[:]), dk_sb[b][:])
            nc.sync.dma_start(out[b * P : (b + 1) * P, :], windows[b][:])
